import numpy as np
import ml_dtypes

BF16 = ml_dtypes.bfloat16


def bf(x):
    return np.asarray(x, np.float32).astype(BF16)


def f32(x):
    return np.asarray(x, np.float32)


def f64(x):
    return np.asarray(x).astype(np.float64)


def striped(idx):
    return np.tile(idx.reshape(-1, 16).T, (8, 1))


S, K, M, N, E, Q = 512, 128, 256, 128, 2, 64


def setup_inputs():
    return {"base": bf(np.random.standard_normal((M, S))), "x": bf(np.random.standard_normal((K, N))), "w": bf(np.random.standard_normal((E, K, M)) / np.sqrt(K)), "c": f32(0.2 + 0.8 * np.random.random_sample((1, S))), "offs": striped(np.random.permutation(S)[:N])}


def reference(base, x, w, c, offs):
    idx = offs[:16].T.reshape(-1)
    z = f64(base).copy()
    for e in range(E):
        z[:, idx[e * Q : (e + 1) * Q]] = f64(w)[e].T @ f64(x)[:, e * Q : (e + 1) * Q]
    return z * f64(c)

@@ -1,0 +1,61 @@
+import concourse.mybir as mybir
+from concourse.masks import make_identity
+
+BF16, F32, U16 = mybir.dt.bfloat16, mybir.dt.float32, mybir.dt.uint16
+
+P = 128
+TOKENS = 512
+FEATURES = 256
+LIST = 128
+EXPERTS = 2
+PIECE = LIST // EXPERTS
+PIECE_COLS = PIECE // 16
+BLOCKS = FEATURES // P
+
+FLOPS = 2 * P * FEATURES * LIST
+
+
+def tile_scatter_matmul_kernel(tc, base, x, w, c, offs, out):
+    nc = tc.nc
+    with (
+        tc.tile_pool(name="held", bufs=1) as held,
+        tc.psum_pool(name="psum", bufs=1) as psum,
+    ):
+        base_tiles = [held.tile([P, TOKENS], BF16, name=f"base{b}") for b in range(BLOCKS)]
+        nc.sync.dma_start(base_tiles[0][:], base[0:P, :])
+        nc.scalar.dma_start(base_tiles[1][:], base[P : 2 * P, :])
+
+        offsets = held.tile([P, LIST // 16], U16, name="offsets")
+        nc.sync.dma_start(offsets[:], offs)
+
+        x_tile = held.tile([P, LIST], BF16, name="x_tile")
+        nc.sync.dma_start(x_tile[:], x)
+
+        w_tile = held.tile([P, EXPERTS, FEATURES], BF16, name="w_tile")
+        nc.scalar.dma_start(w_tile[:], w.rearrange("e k m -> k e m"))
+
+        ident = held.tile([P, P], BF16, name="ident")
+        make_identity(nc, ident[:])
+
+        c_all = held.tile([P, TOKENS], F32, name="c_all")
+        nc.gpsimd.dma_start(c_all[:], c.broadcast_to([P, TOKENS]))
+
+        windows = [psum.tile([P, TOKENS], F32, name=f"window{b}") for b in range(BLOCKS)]
+        for b in range(BLOCKS):
+            nc.tensor.matmul(windows[b][:], ident[:], base_tiles[b][:], start=True, stop=True)
+
+        for b in range(BLOCKS):
+            for e in range(EXPERTS):
+                nc.tensor.matmul(
+                    windows[b][:].indirect(offsets[:, e * PIECE_COLS : (e + 1) * PIECE_COLS]),
+                    w_tile[:, e, b * P : (b + 1) * P],
+                    x_tile[:, e * PIECE : (e + 1) * PIECE],
+                    start=True,
+                    stop=True,
+                )
+
+        for b in range(BLOCKS):
+            scaled = held.tile([P, TOKENS], F32, name=f"scaled{b}")
+            nc.vector.tensor_tensor(scaled[:], windows[b][:], c_all[:], mybir.AluOpType.mult)
+            store_queue = nc.sync if b % 2 == 0 else nc.scalar
+            store_queue.dma_start(out[b * P : (b + 1) * P, :], scaled[:])

@@ -29,16 +29,16 @@ def tile_scatter_matmul_kernel(tc, base, x, w, c, offs, out):
         nc.sync.dma_start(offsets[:], offs)
 
         x_tile = held.tile([P, LIST], BF16, name="x_tile")
-        nc.sync.dma_start(x_tile[:], x)
+        nc.scalar.dma_start(x_tile[:], x)
 
         w_tile = held.tile([P, EXPERTS, FEATURES], BF16, name="w_tile")
-        nc.scalar.dma_start(w_tile[:], w.rearrange("e k m -> k e m"))
+        nc.sync.dma_start(w_tile[:], w.rearrange("e k m -> k e m"))
 
         ident = held.tile([P, P], BF16, name="ident")
         make_identity(nc, ident[:])
 
         c_all = held.tile([P, TOKENS], F32, name="c_all")
-        nc.gpsimd.dma_start(c_all[:], c.broadcast_to([P, TOKENS]))
+        nc.scalar.dma_start(c_all[:], c.broadcast_to([P, TOKENS]))
 
         windows = [psum.tile([P, TOKENS], F32, name=f"window{b}") for b in range(BLOCKS)]
         for b in range(BLOCKS):

@@ -11,6 +11,7 @@ EXPERTS = 2
 PIECE = LIST // EXPERTS
 PIECE_COLS = PIECE // 16
 BLOCKS = FEATURES // P
+HALF = TOKENS // 2
 
 FLOPS = 2 * P * FEATURES * LIST
 
@@ -37,8 +38,9 @@ def tile_scatter_matmul_kernel(tc, base, x, w, c, offs, out):
         ident = held.tile([P, P], BF16, name="ident")
         make_identity(nc, ident[:])
 
-        c_all = held.tile([P, TOKENS], F32, name="c_all")
-        nc.scalar.dma_start(c_all[:], c.broadcast_to([P, TOKENS]))
+        c_halves = [held.tile([P, HALF], F32, name=f"c_half{h}") for h in range(2)]
+        for h in range(2):
+            nc.scalar.dma_start(c_halves[h][:], c[:, h * HALF : (h + 1) * HALF].broadcast_to([P, HALF]))
 
         windows = [psum.tile([P, TOKENS], F32, name=f"window{b}") for b in range(BLOCKS)]
         for b in range(BLOCKS):
@@ -54,8 +56,10 @@ def tile_scatter_matmul_kernel(tc, base, x, w, c, offs, out):
                     stop=True,
                 )
 
-        for b in range(BLOCKS):
-            scaled = held.tile([P, TOKENS], F32, name=f"scaled{b}")
-            nc.vector.tensor_tensor(scaled[:], windows[b][:], c_all[:], mybir.AluOpType.mult)
-            store_queue = nc.sync if b % 2 == 0 else nc.scalar
-            store_queue.dma_start(out[b * P : (b + 1) * P, :], scaled[:])
+        for h in range(2):
+            cols = slice(h * HALF, (h + 1) * HALF)
+            for b in range(BLOCKS):
+                scaled = held.tile([P, HALF], F32, name=f"scaled{b}_{h}")
+                nc.vector.tensor_tensor(scaled[:], windows[b][:, cols], c_halves[h][:], mybir.AluOpType.mult)
+                store_queue = nc.sync if b % 2 == 0 else nc.scalar
+                store_queue.dma_start(out[b * P : (b + 1) * P, cols], scaled[:])

@@ -11,7 +11,8 @@ EXPERTS = 2
 PIECE = LIST // EXPERTS
 PIECE_COLS = PIECE // 16
 BLOCKS = FEATURES // P
-HALF = TOKENS // 2
+
+WARM_UPS = 3
 
 FLOPS = 2 * P * FEATURES * LIST
 
@@ -38,9 +39,14 @@ def tile_scatter_matmul_kernel(tc, base, x, w, c, offs, out):
         ident = held.tile([P, P], BF16, name="ident")
         make_identity(nc, ident[:])
 
-        c_halves = [held.tile([P, HALF], F32, name=f"c_half{h}") for h in range(2)]
-        for h in range(2):
-            nc.scalar.dma_start(c_halves[h][:], c[:, h * HALF : (h + 1) * HALF].broadcast_to([P, HALF]))
+        c_all = held.tile([P, TOKENS], F32, name="c_all")
+        nc.scalar.dma_start(c_all[:], c.broadcast_to([P, TOKENS]))
+
+        zeros = held.tile([P, TOKENS], BF16, name="zeros")
+        nc.vector.memset(zeros[:], 0.0)
+        unread = psum.tile([P, TOKENS], F32, name="unread")
+        for i in range(WARM_UPS):
+            nc.tensor.matmul(unread[:], zeros[:, 0:P], zeros[:], start=True, stop=True)
 
         windows = [psum.tile([P, TOKENS], F32, name=f"window{b}") for b in range(BLOCKS)]
         for b in range(BLOCKS):
@@ -56,10 +62,8 @@ def tile_scatter_matmul_kernel(tc, base, x, w, c, offs, out):
                     stop=True,
                 )
 
-        for h in range(2):
-            cols = slice(h * HALF, (h + 1) * HALF)
-            for b in range(BLOCKS):
-                scaled = held.tile([P, HALF], F32, name=f"scaled{b}_{h}")
-                nc.vector.tensor_tensor(scaled[:], windows[b][:, cols], c_halves[h][:], mybir.AluOpType.mult)
-                store_queue = nc.sync if b % 2 == 0 else nc.scalar
-                store_queue.dma_start(out[b * P : (b + 1) * P, cols], scaled[:])
+        for b in range(BLOCKS):
+            scaled = held.tile([P, TOKENS], F32, name=f"scaled{b}")
+            nc.vector.tensor_tensor(scaled[:], windows[b][:], c_all[:], mybir.AluOpType.mult)
+            store_queue = nc.sync if b % 2 == 0 else nc.scalar
+            store_queue.dma_start(out[b * P : (b + 1) * P, :], scaled[:])

@@ -11,6 +11,7 @@ EXPERTS = 2
 PIECE = LIST // EXPERTS
 PIECE_COLS = PIECE // 16
 BLOCKS = FEATURES // P
+PER_PARTITION = TOKENS // P
 
 WARM_UPS = 3
 
@@ -23,6 +24,9 @@ def tile_scatter_matmul_kernel(tc, base, x, w, c, offs, out):
         tc.tile_pool(name="held", bufs=1) as held,
         tc.psum_pool(name="psum", bufs=1) as psum,
     ):
+        c_cols = held.tile([P, PER_PARTITION], F32, name="c_cols")
+        nc.scalar.dma_start(c_cols[:], c.rearrange("o (p a) -> p (o a)", a=PER_PARTITION))
+
         base_tiles = [held.tile([P, TOKENS], BF16, name=f"base{b}") for b in range(BLOCKS)]
         nc.sync.dma_start(base_tiles[0][:], base[0:P, :])
         nc.scalar.dma_start(base_tiles[1][:], base[P : 2 * P, :])
@@ -36,17 +40,29 @@ def tile_scatter_matmul_kernel(tc, base, x, w, c, offs, out):
         w_tile = held.tile([P, EXPERTS, FEATURES], BF16, name="w_tile")
         nc.sync.dma_start(w_tile[:], w.rearrange("e k m -> k e m"))
 
+        ident_f32 = held.tile([P, P], F32, name="ident_f32")
+        make_identity(nc, ident_f32[:])
         ident = held.tile([P, P], BF16, name="ident")
-        make_identity(nc, ident[:])
-
-        c_all = held.tile([P, TOKENS], F32, name="c_all")
-        nc.scalar.dma_start(c_all[:], c.broadcast_to([P, TOKENS]))
+        nc.vector.tensor_copy(ident[:], ident_f32[:])
 
         zeros = held.tile([P, TOKENS], BF16, name="zeros")
         nc.vector.memset(zeros[:], 0.0)
         unread = psum.tile([P, TOKENS], F32, name="unread")
         for i in range(WARM_UPS):
             nc.tensor.matmul(unread[:], zeros[:, 0:P], zeros[:], start=True, stop=True)
+
+        c_spread = psum.tile([P, TOKENS], F32, name="c_spread")
+        for a in range(PER_PARTITION):
+            nc.tensor.transpose(
+                c_spread[:, a * P : (a + 1) * P],
+                c_cols[:, a : a + 1].to_broadcast([P, P]),
+                ident_f32[:],
+            )
+        c_all = held.tile([P, TOKENS], F32, name="c_all")
+        nc.vector.tensor_copy(
+            c_all[:].rearrange("m (p a) -> m p a", a=PER_PARTITION),
+            c_spread[:].rearrange("m (a p) -> m p a", a=PER_PARTITION),
+        )
 
         windows = [psum.tile([P, TOKENS], F32, name=f"window{b}") for b in range(BLOCKS)]
         for b in range(BLOCKS):

@@ -13,7 +13,7 @@ PIECE_COLS = PIECE // 16
 BLOCKS = FEATURES // P
 PER_PARTITION = TOKENS // P
 
-WARM_UPS = 3
+WARM_UPS = 12
 
 FLOPS = 2 * P * FEATURES * LIST
 
@@ -45,11 +45,11 @@ def tile_scatter_matmul_kernel(tc, base, x, w, c, offs, out):
         ident = held.tile([P, P], BF16, name="ident")
         nc.vector.tensor_copy(ident[:], ident_f32[:])
 
-        zeros = held.tile([P, TOKENS], BF16, name="zeros")
+        zeros = held.tile([P, P], BF16, name="zeros")
         nc.vector.memset(zeros[:], 0.0)
-        unread = psum.tile([P, TOKENS], F32, name="unread")
+        unread = psum.tile([P, P], F32, name="unread")
         for i in range(WARM_UPS):
-            nc.tensor.matmul(unread[:], zeros[:, 0:P], zeros[:], start=True, stop=True)
+            nc.tensor.matmul(unread[:], zeros[:], zeros[:], start=True, stop=True)
 
         c_spread = psum.tile([P, TOKENS], F32, name="c_spread")
         for a in range(PER_PARTITION):

@@ -41,7 +41,8 @@ def tile_scatter_matmul_kernel(tc, base, x, w, c, offs, out):
         nc.sync.dma_start(w_tile[:], w.rearrange("e k m -> k e m"))
 
         ident_f32 = held.tile([P, P], F32, name="ident_f32")
-        make_identity(nc, ident_f32[:])
+        nc.vector.memset(ident_f32[:], 0.0)
+        make_identity(nc, ident_f32[:], nomemset=True)
         ident = held.tile([P, P], BF16, name="ident")
         nc.vector.tensor_copy(ident[:], ident_f32[:])
 

@@ -25,20 +25,20 @@ def tile_scatter_matmul_kernel(tc, base, x, w, c, offs, out):
         tc.psum_pool(name="psum", bufs=1) as psum,
     ):
         c_cols = held.tile([P, PER_PARTITION], F32, name="c_cols")
-        nc.scalar.dma_start(c_cols[:], c.rearrange("o (p a) -> p (o a)", a=PER_PARTITION))
+        nc.sync.dma_start(c_cols[:], c.rearrange("o (p a) -> p (o a)", a=PER_PARTITION))
 
         base_tiles = [held.tile([P, TOKENS], BF16, name=f"base{b}") for b in range(BLOCKS)]
-        nc.sync.dma_start(base_tiles[0][:], base[0:P, :])
-        nc.scalar.dma_start(base_tiles[1][:], base[P : 2 * P, :])
+        nc.scalar.dma_start(base_tiles[0][:], base[0:P, :])
+        nc.sync.dma_start(base_tiles[1][:], base[P : 2 * P, :])
+
+        w_tile = held.tile([P, EXPERTS, FEATURES], BF16, name="w_tile")
+        nc.scalar.dma_start(w_tile[:], w.rearrange("e k m -> k e m"))
 
         offsets = held.tile([P, LIST // 16], U16, name="offsets")
         nc.sync.dma_start(offsets[:], offs)
 
         x_tile = held.tile([P, LIST], BF16, name="x_tile")
         nc.scalar.dma_start(x_tile[:], x)
-
-        w_tile = held.tile([P, EXPERTS, FEATURES], BF16, name="w_tile")
-        nc.sync.dma_start(w_tile[:], w.rearrange("e k m -> k e m"))
 
         ident_f32 = held.tile([P, P], F32, name="ident_f32")
         nc.vector.memset(ident_f32[:], 0.0)

@@ -13,7 +13,7 @@ PIECE_COLS = PIECE // 16
 BLOCKS = FEATURES // P
 PER_PARTITION = TOKENS // P
 
-WARM_UPS = 12
+WARM_UPS = 14
 
 FLOPS = 2 * P * FEATURES * LIST
 
@@ -24,6 +24,13 @@ def tile_scatter_matmul_kernel(tc, base, x, w, c, offs, out):
         tc.tile_pool(name="held", bufs=1) as held,
         tc.psum_pool(name="psum", bufs=1) as psum,
     ):
+        zeros = held.tile([P, 2], BF16, name="zeros")
+        nc.vector.memset(zeros[:], 0.0)
+        zero_block = zeros[:, 0:1].to_broadcast([P, P])
+        unread = psum.tile([P, P], F32, name="unread")
+        for i in range(WARM_UPS):
+            nc.tensor.matmul(unread[:], zero_block, zero_block, start=True, stop=True)
+
         c_cols = held.tile([P, PER_PARTITION], F32, name="c_cols")
         nc.sync.dma_start(c_cols[:], c.rearrange("o (p a) -> p (o a)", a=PER_PARTITION))
 
@@ -45,12 +52,6 @@ def tile_scatter_matmul_kernel(tc, base, x, w, c, offs, out):
         make_identity(nc, ident_f32[:], nomemset=True)
         ident = held.tile([P, P], BF16, name="ident")
         nc.vector.tensor_copy(ident[:], ident_f32[:])
-
-        zeros = held.tile([P, P], BF16, name="zeros")
-        nc.vector.memset(zeros[:], 0.0)
-        unread = psum.tile([P, P], F32, name="unread")
-        for i in range(WARM_UPS):
-            nc.tensor.matmul(unread[:], zeros[:], zeros[:], start=True, stop=True)
 
         c_spread = psum.tile([P, TOKENS], F32, name="c_spread")
         for a in range(PER_PARTITION):

@@ -13,7 +13,7 @@ PIECE_COLS = PIECE // 16
 BLOCKS = FEATURES // P
 PER_PARTITION = TOKENS // P
 
-WARM_UPS = 14
+WARM_UPS = 10
 
 FLOPS = 2 * P * FEATURES * LIST
 

@@ -45,7 +45,7 @@ def tile_scatter_matmul_kernel(tc, base, x, w, c, offs, out):
         nc.sync.dma_start(offsets[:], offs)
 
         x_tile = held.tile([P, LIST], BF16, name="x_tile")
-        nc.scalar.dma_start(x_tile[:], x)
+        nc.sync.dma_start(x_tile[:], x)
 
         ident_f32 = held.tile([P, P], F32, name="ident_f32")
         nc.vector.memset(ident_f32[:], 0.0)

@@ -83,5 +83,4 @@ def tile_scatter_matmul_kernel(tc, base, x, w, c, offs, out):
         for b in range(BLOCKS):
             scaled = held.tile([P, TOKENS], F32, name=f"scaled{b}")
             nc.vector.tensor_tensor(scaled[:], windows[b][:], c_all[:], mybir.AluOpType.mult)
-            store_queue = nc.sync if b % 2 == 0 else nc.scalar
-            store_queue.dma_start(out[b * P : (b + 1) * P, :], scaled[:])
+            nc.scalar.dma_start(out[b * P : (b + 1) * P, :], scaled[:])

@@ -34,18 +34,18 @@ def tile_scatter_matmul_kernel(tc, base, x, w, c, offs, out):
         c_cols = held.tile([P, PER_PARTITION], F32, name="c_cols")
         nc.sync.dma_start(c_cols[:], c.rearrange("o (p a) -> p (o a)", a=PER_PARTITION))
 
+        offsets = held.tile([P, LIST // 16], U16, name="offsets")
+        nc.sync.dma_start(offsets[:], offs)
+
         base_tiles = [held.tile([P, TOKENS], BF16, name=f"base{b}") for b in range(BLOCKS)]
-        nc.scalar.dma_start(base_tiles[0][:], base[0:P, :])
-        nc.sync.dma_start(base_tiles[1][:], base[P : 2 * P, :])
+        for b in range(BLOCKS):
+            nc.scalar.dma_start(base_tiles[b][:], base[b * P : (b + 1) * P, :])
 
         w_tile = held.tile([P, EXPERTS, FEATURES], BF16, name="w_tile")
         nc.scalar.dma_start(w_tile[:], w.rearrange("e k m -> k e m"))
 
-        offsets = held.tile([P, LIST // 16], U16, name="offsets")
-        nc.sync.dma_start(offsets[:], offs)
-
         x_tile = held.tile([P, LIST], BF16, name="x_tile")
-        nc.sync.dma_start(x_tile[:], x)
+        nc.scalar.dma_start(x_tile[:], x)
 
         ident_f32 = held.tile([P, P], F32, name="ident_f32")
         nc.vector.memset(ident_f32[:], 0.0)
@@ -83,4 +83,4 @@ def tile_scatter_matmul_kernel(tc, base, x, w, c, offs, out):
         for b in range(BLOCKS):
             scaled = held.tile([P, TOKENS], F32, name=f"scaled{b}")
             nc.vector.tensor_tensor(scaled[:], windows[b][:], c_all[:], mybir.AluOpType.mult)
-            nc.scalar.dma_start(out[b * P : (b + 1) * P, :], scaled[:])
+            nc.sync.dma_start(out[b * P : (b + 1) * P, :], scaled[:])

@@ -37,9 +37,8 @@ def tile_scatter_matmul_kernel(tc, base, x, w, c, offs, out):
         offsets = held.tile([P, LIST // 16], U16, name="offsets")
         nc.sync.dma_start(offsets[:], offs)
 
-        base_tiles = [held.tile([P, TOKENS], BF16, name=f"base{b}") for b in range(BLOCKS)]
-        for b in range(BLOCKS):
-            nc.scalar.dma_start(base_tiles[b][:], base[b * P : (b + 1) * P, :])
+        base_tile = held.tile([P, BLOCKS, TOKENS], BF16, name="base_tile")
+        nc.scalar.dma_start(base_tile[:], base.rearrange("(b p) t -> p b t", b=BLOCKS))
 
         w_tile = held.tile([P, EXPERTS, FEATURES], BF16, name="w_tile")
         nc.scalar.dma_start(w_tile[:], w.rearrange("e k m -> k e m"))
@@ -68,7 +67,7 @@ def tile_scatter_matmul_kernel(tc, base, x, w, c, offs, out):
 
         windows = [psum.tile([P, TOKENS], F32, name=f"window{b}") for b in range(BLOCKS)]
         for b in range(BLOCKS):
-            nc.tensor.matmul(windows[b][:], ident[:], base_tiles[b][:], start=True, stop=True)
+            nc.tensor.matmul(windows[b][:], ident[:], base_tile[:, b, :], start=True, stop=True)
 
         for b in range(BLOCKS):
             for e in range(EXPERTS):

@@ -40,11 +40,12 @@ def tile_scatter_matmul_kernel(tc, base, x, w, c, offs, out):
         base_tile = held.tile([P, BLOCKS, TOKENS], BF16, name="base_tile")
         nc.scalar.dma_start(base_tile[:], base.rearrange("(b p) t -> p b t", b=BLOCKS))
 
-        w_tile = held.tile([P, EXPERTS, FEATURES], BF16, name="w_tile")
-        nc.scalar.dma_start(w_tile[:], w.rearrange("e k m -> k e m"))
-
         x_tile = held.tile([P, LIST], BF16, name="x_tile")
         nc.scalar.dma_start(x_tile[:], x)
+
+        w_tiles = [held.tile([P, FEATURES], BF16, name=f"w{e}") for e in range(EXPERTS)]
+        for e in range(EXPERTS):
+            nc.scalar.dma_start(w_tiles[e][:], w[e])
 
         ident_f32 = held.tile([P, P], F32, name="ident_f32")
         nc.vector.memset(ident_f32[:], 0.0)
@@ -69,11 +70,11 @@ def tile_scatter_matmul_kernel(tc, base, x, w, c, offs, out):
         for b in range(BLOCKS):
             nc.tensor.matmul(windows[b][:], ident[:], base_tile[:, b, :], start=True, stop=True)
 
-        for b in range(BLOCKS):
-            for e in range(EXPERTS):
+        for e in range(EXPERTS):
+            for b in range(BLOCKS):
                 nc.tensor.matmul(
                     windows[b][:].indirect(offsets[:, e * PIECE_COLS : (e + 1) * PIECE_COLS]),
-                    w_tile[:, e, b * P : (b + 1) * P],
+                    w_tiles[e][:, b * P : (b + 1) * P],
                     x_tile[:, e * PIECE : (e + 1) * PIECE],
                     start=True,
                     stop=True,

@@ -70,8 +70,8 @@ def tile_scatter_matmul_kernel(tc, base, x, w, c, offs, out):
         for b in range(BLOCKS):
             nc.tensor.matmul(windows[b][:], ident[:], base_tile[:, b, :], start=True, stop=True)
 
-        for e in range(EXPERTS):
-            for b in range(BLOCKS):
+        for b in range(BLOCKS):
+            for e in range(EXPERTS):
                 nc.tensor.matmul(
                     windows[b][:].indirect(offsets[:, e * PIECE_COLS : (e + 1) * PIECE_COLS]),
                     w_tiles[e][:, b * P : (b + 1) * P],

@@ -13,7 +13,8 @@ PIECE_COLS = PIECE // 16
 BLOCKS = FEATURES // P
 PER_PARTITION = TOKENS // P
 
-WARM_UPS = 10
+WARM_UP_WIDTH = 256
+WARM_UPS = 5
 
 FLOPS = 2 * P * FEATURES * LIST
 
@@ -26,10 +27,11 @@ def tile_scatter_matmul_kernel(tc, base, x, w, c, offs, out):
     ):
         zeros = held.tile([P, 2], BF16, name="zeros")
         nc.vector.memset(zeros[:], 0.0)
-        zero_block = zeros[:, 0:1].to_broadcast([P, P])
-        unread = psum.tile([P, P], F32, name="unread")
+        zero_weights = zeros[:, 0:1].to_broadcast([P, P])
+        zero_columns = zeros[:, 0:1].to_broadcast([P, WARM_UP_WIDTH])
+        unread = psum.tile([P, WARM_UP_WIDTH], F32, name="unread")
         for i in range(WARM_UPS):
-            nc.tensor.matmul(unread[:], zero_block, zero_block, start=True, stop=True)
+            nc.tensor.matmul(unread[:], zero_weights, zero_columns, start=True, stop=True)
 
         c_cols = held.tile([P, PER_PARTITION], F32, name="c_cols")
         nc.sync.dma_start(c_cols[:], c.rearrange("o (p a) -> p (o a)", a=PER_PARTITION))

@@ -13,6 +13,8 @@ PIECE_COLS = PIECE // 16
 BLOCKS = FEATURES // P
 PER_PARTITION = TOKENS // P
 
+BURST = 256
+
 WARM_UP_WIDTH = 256
 WARM_UPS = 5
 
@@ -39,13 +41,13 @@ def tile_scatter_matmul_kernel(tc, base, x, w, c, offs, out):
         offsets = held.tile([P, LIST // 16], U16, name="offsets")
         nc.sync.dma_start(offsets[:], offs)
 
-        base_tile = held.tile([P, BLOCKS, TOKENS], BF16, name="base_tile")
+        base_tile = held.tile([P, BLOCKS, TOKENS], BF16, name="base_tile", align_bytes=BURST)
         nc.scalar.dma_start(base_tile[:], base.rearrange("(b p) t -> p b t", b=BLOCKS))
 
-        x_tile = held.tile([P, LIST], BF16, name="x_tile")
+        x_tile = held.tile([P, LIST], BF16, name="x_tile", align_bytes=BURST)
         nc.scalar.dma_start(x_tile[:], x)
 
-        w_tiles = [held.tile([P, FEATURES], BF16, name=f"w{e}") for e in range(EXPERTS)]
+        w_tiles = [held.tile([P, FEATURES], BF16, name=f"w{e}", align_bytes=BURST) for e in range(EXPERTS)]
         for e in range(EXPERTS):
             nc.scalar.dma_start(w_tiles[e][:], w[e])
 
@@ -83,6 +85,6 @@ def tile_scatter_matmul_kernel(tc, base, x, w, c, offs, out):
                 )
 
         for b in range(BLOCKS):
-            scaled = held.tile([P, TOKENS], F32, name=f"scaled{b}")
+            scaled = held.tile([P, TOKENS], F32, name=f"scaled{b}", align_bytes=BURST)
             nc.vector.tensor_tensor(scaled[:], windows[b][:], c_all[:], mybir.AluOpType.mult)
             nc.sync.dma_start(out[b * P : (b + 1) * P, :], scaled[:])

@@ -18,6 +18,9 @@ BURST = 256
 WARM_UP_WIDTH = 256
 WARM_UPS = 5
 
+ARRAY_TILE = 32
+SLICE = 64
+
 FLOPS = 2 * P * FEATURES * LIST
 
 
@@ -41,15 +44,13 @@ def tile_scatter_matmul_kernel(tc, base, x, w, c, offs, out):
         offsets = held.tile([P, LIST // 16], U16, name="offsets")
         nc.sync.dma_start(offsets[:], offs)
 
-        base_tile = held.tile([P, BLOCKS, TOKENS], BF16, name="base_tile", align_bytes=BURST)
-        nc.scalar.dma_start(base_tile[:], base.rearrange("(b p) t -> p b t", b=BLOCKS))
-
+        base_tiles = [held.tile([P, TOKENS], BF16, name=f"base{b}", align_bytes=BURST) for b in range(BLOCKS)]
         x_tile = held.tile([P, LIST], BF16, name="x_tile", align_bytes=BURST)
+        w_tile = held.tile([P, EXPERTS, FEATURES], BF16, name="w_tile", align_bytes=BURST)
+        nc.scalar.dma_start(base_tiles[0][:], base[0:P, :])
         nc.scalar.dma_start(x_tile[:], x)
-
-        w_tiles = [held.tile([P, FEATURES], BF16, name=f"w{e}", align_bytes=BURST) for e in range(EXPERTS)]
-        for e in range(EXPERTS):
-            nc.scalar.dma_start(w_tiles[e][:], w[e])
+        nc.scalar.dma_start(w_tile[:], w.rearrange("e k m -> k e m"))
+        nc.scalar.dma_start(base_tiles[1][:], base[P : 2 * P, :])
 
         ident_f32 = held.tile([P, P], F32, name="ident_f32")
         nc.vector.memset(ident_f32[:], 0.0)
@@ -71,18 +72,30 @@ def tile_scatter_matmul_kernel(tc, base, x, w, c, offs, out):
         )
 
         windows = [psum.tile([P, TOKENS], F32, name=f"window{b}") for b in range(BLOCKS)]
-        for b in range(BLOCKS):
-            nc.tensor.matmul(windows[b][:], ident[:], base_tile[:, b, :], start=True, stop=True)
 
-        for b in range(BLOCKS):
+        def place_products(b):
             for e in range(EXPERTS):
                 nc.tensor.matmul(
                     windows[b][:].indirect(offsets[:, e * PIECE_COLS : (e + 1) * PIECE_COLS]),
-                    w_tiles[e][:, b * P : (b + 1) * P],
+                    w_tile[:, e, b * P : (b + 1) * P],
                     x_tile[:, e * PIECE : (e + 1) * PIECE],
                     start=True,
                     stop=True,
                 )
+
+        nc.tensor.matmul(windows[0][:], ident[:], base_tiles[0][:], start=True, stop=True)
+        place_products(0)
+
+        for first_token in range(0, TOKENS, SLICE):
+            for first in range(0, P, ARRAY_TILE):
+                nc.tensor.matmul(
+                    windows[1][first : first + ARRAY_TILE, first_token : first_token + SLICE],
+                    ident[:, first : first + ARRAY_TILE],
+                    base_tiles[1][:, first_token : first_token + SLICE],
+                    start=True,
+                    stop=True,
+                )
+        place_products(1)
 
         for b in range(BLOCKS):
             scaled = held.tile([P, TOKENS], F32, name=f"scaled{b}", align_bytes=BURST)

import concourse.mybir as mybir
from concourse.masks import make_identity

BF16, F32, U16 = mybir.dt.bfloat16, mybir.dt.float32, mybir.dt.uint16

P = 128
TOKENS = 512
FEATURES = 256
LIST = 128
EXPERTS = 2
PIECE = LIST // EXPERTS
PIECE_COLS = PIECE // 16
BLOCKS = FEATURES // P
PER_PARTITION = TOKENS // P

BURST = 256

WARM_UP_WIDTH = 256
WARM_UPS = 5

ARRAY_TILE = 32
SLICE = 64

FLOPS = 2 * P * FEATURES * LIST


def tile_scatter_matmul_kernel(tc, base, x, w, c, offs, out):
    nc = tc.nc
    with (
        tc.tile_pool(name="held", bufs=1) as held,
        tc.psum_pool(name="psum", bufs=1) as psum,
    ):
        zeros = held.tile([P, 2], BF16, name="zeros")
        nc.vector.memset(zeros[:], 0.0)
        zero_weights = zeros[:, 0:1].to_broadcast([P, P])
        zero_columns = zeros[:, 0:1].to_broadcast([P, WARM_UP_WIDTH])
        unread = psum.tile([P, WARM_UP_WIDTH], F32, name="unread")
        for i in range(WARM_UPS):
            nc.tensor.matmul(unread[:], zero_weights, zero_columns, start=True, stop=True)

        c_cols = held.tile([P, PER_PARTITION], F32, name="c_cols")
        nc.sync.dma_start(c_cols[:], c.rearrange("o (p a) -> p (o a)", a=PER_PARTITION))

        offsets = held.tile([P, LIST // 16], U16, name="offsets")
        nc.sync.dma_start(offsets[:], offs)

        base_tiles = [held.tile([P, TOKENS], BF16, name=f"base{b}", align_bytes=BURST) for b in range(BLOCKS)]
        x_tile = held.tile([P, LIST], BF16, name="x_tile", align_bytes=BURST)
        w_tile = held.tile([P, EXPERTS, FEATURES], BF16, name="w_tile", align_bytes=BURST)
        nc.scalar.dma_start(base_tiles[0][:], base[0:P, :])
        nc.scalar.dma_start(x_tile[:], x)
        nc.scalar.dma_start(w_tile[:], w.rearrange("e k m -> k e m"))
        nc.scalar.dma_start(base_tiles[1][:], base[P : 2 * P, :])

        ident_f32 = held.tile([P, P], F32, name="ident_f32")
        nc.vector.memset(ident_f32[:], 0.0)
        make_identity(nc, ident_f32[:], nomemset=True)
        ident = held.tile([P, P], BF16, name="ident")
        nc.vector.tensor_copy(ident[:], ident_f32[:])

        c_spread = psum.tile([P, TOKENS], F32, name="c_spread")
        for a in range(PER_PARTITION):
            nc.tensor.transpose(
                c_spread[:, a * P : (a + 1) * P],
                c_cols[:, a : a + 1].to_broadcast([P, P]),
                ident_f32[:],
            )
        c_all = held.tile([P, TOKENS], F32, name="c_all")
        nc.vector.tensor_copy(
            c_all[:].rearrange("m (p a) -> m p a", a=PER_PARTITION),
            c_spread[:].rearrange("m (a p) -> m p a", a=PER_PARTITION),
        )

        windows = [psum.tile([P, TOKENS], F32, name=f"window{b}") for b in range(BLOCKS)]

        def place_products(b):
            for e in range(EXPERTS):
                nc.tensor.matmul(
                    windows[b][:].indirect(offsets[:, e * PIECE_COLS : (e + 1) * PIECE_COLS]),
                    w_tile[:, e, b * P : (b + 1) * P],
                    x_tile[:, e * PIECE : (e + 1) * PIECE],
                    start=True,
                    stop=True,
                )

        nc.tensor.matmul(windows[0][:], ident[:], base_tiles[0][:], start=True, stop=True)
        place_products(0)

        for first_token in range(0, TOKENS, SLICE):
            for first in range(0, P, ARRAY_TILE):
                nc.tensor.matmul(
                    windows[1][first : first + ARRAY_TILE, first_token : first_token + SLICE],
                    ident[:, first : first + ARRAY_TILE],
                    base_tiles[1][:, first_token : first_token + SLICE],
                    start=True,
                    stop=True,
                )
        place_products(1)

        for b in range(BLOCKS):
            scaled = held.tile([P, TOKENS], F32, name=f"scaled{b}", align_bytes=BURST)
            nc.vector.tensor_tensor(scaled[:], windows[b][:], c_all[:], mybir.AluOpType.mult)
            nc.sync.dma_start(out[b * P : (b + 1) * P, :], scaled[:])
